import numpy as np
import ml_dtypes


def mxq(x, axis, fmt="e4m3"):
    dtype, down = {"e4m3": (ml_dtypes.float8_e4m3fn, 7), "e5m2": (ml_dtypes.float8_e5m2, 14)}[fmt]
    v = np.moveaxis(np.asarray(x, np.float32).astype(ml_dtypes.bfloat16).astype(np.float64), axis, -1)
    blocks = v.reshape(v.shape[:-1] + (-1, 32))
    amax = np.abs(blocks).max(-1, keepdims=True)
    byte = np.maximum(np.where(amax > 0, np.frexp(amax)[1] - 1 + 127, 0) - down, 1)
    scale = np.exp2(byte - 127.0)
    codes = (blocks / scale).astype(np.float32).astype(dtype).astype(np.float64)
    return np.moveaxis((codes * scale).reshape(v.shape), -1, axis)


WIDE = False


def mx_kscale(k):
    if not WIDE:
        return np.ones(k)
    levels = np.array([10, -10, 5, -5, 0])
    if k % 512:
        return np.exp2(np.random.permutation(np.resize(levels, k // 32))).repeat(32)
    a = np.empty((k // 512, 16))
    for p in range(k // 512):
        a[p, :8] = np.random.permutation(np.resize(levels, 8))
        for g in range(8):
            far = levels[np.abs(levels - a[p, g]) >= 10]
            a[p, g + 8] = far[np.random.randint(len(far))]
    return np.exp2(a.ravel()).repeat(32)


BF16 = ml_dtypes.bfloat16


def bf(x):
    return np.asarray(x, np.float32).astype(BF16)


def f64(x):
    return np.asarray(x).astype(np.float64)


P, N, S = 1024, 2048, 1024


def draw0():
    s, t = mx_kscale(N), mx_kscale(P)
    member = np.random.random((P, N)) < 0.5
    volume = member * (0.5 + np.random.random((P, N)))
    trust = member * (0.5 + np.random.random((P, N)))
    lognegs = 2.0 * np.random.standard_normal((N, S)) / np.sqrt(N)
    return {"design": bf(volume * s),
            "lognegs": bf(lognegs / s[:, None]),
            "midpoint": bf(0.5 * np.random.standard_normal(P)),
            "readout": bf(np.random.standard_normal((P, S)) * t[:, None]),
            "back": bf(2.0 * trust / np.sqrt(P) / t[:, None])}


def core(design, lognegs, midpoint, readout, back):
    z = mxq(f64(design), 1, "e4m3") @ mxq(f64(lognegs), 0, "e4m3")
    v = 1.0 / (1.0 + np.exp(-(z + f64(midpoint)[:, None])))
    h = v * f64(readout)
    e = mxq(f64(back), 0, "e4m3").T @ mxq(h, 0, "e4m3")
    return e


def e4m3fn_bytes(y):
    return np.clip(np.asarray(y, np.float64), -448.0, 448.0).astype(np.float32).astype(ml_dtypes.float8_e4m3fn).view(np.uint8)


def e4m3fn_values(b):
    return np.asarray(b, np.uint8).view(ml_dtypes.float8_e4m3fn).astype(np.float64)


def setup_inputs():
    d = draw0()
    x0 = np.asarray(d['lognegs']).astype(np.float64)
    s = (np.max(np.abs(x0), axis=(1,), keepdims=True) / 448.0).astype(np.float32)
    out = {}
    for k, v in d.items():
        if k == 'lognegs':
            out['lognegs_bytes'] = e4m3fn_bytes(x0 / s.astype(np.float64))
            out['lognegs_scale'] = s
        else:
            out[k] = v
    return out


def reference(design, lognegs_bytes, lognegs_scale, midpoint, readout, back):
    return core(design, e4m3fn_values(lognegs_bytes) * lognegs_scale.astype(np.float64), midpoint, readout, back)

from contextlib import ExitStack

import concourse.mybir as mybir
from concourse.masks import make_identity

F32 = mybir.dt.float32
BF16 = mybir.dt.bfloat16
U32 = mybir.dt.uint32
U8 = mybir.dt.uint8
FP8 = mybir.dt.float8_e4m3fn
FP8X4 = mybir.dt.float8_e4m3fn_x4
ACT = mybir.ActivationFunctionType
ALU = mybir.AluOpType

POOLS, ITEMS, SCENARIOS = 1024, 2048, 1024
FLOPS = 2 * (2 * POOLS * ITEMS * SCENARIOS)

P = 128
PACK = 4
BANK = 512
ITEM_PASSES = ITEMS // (P * PACK)
POOL_PASSES = POOLS // (P * PACK)
POOL_TILES = POOLS // P
HALVES = SCENARIOS // BANK
GROUP = 4
ITEM_GROUPS = ITEMS // BANK
LAST_ITEM_TILE = ITEMS // P - 1


def tile_pooled_testing_evidence_s7_kernel(
    tc, design, lognegs_bytes, lognegs_scale, midpoint, readout, back, out
):
    nc = tc.nc

    design_rows = design.rearrange("(g p t) k -> g p t k", p=P, t=PACK)
    lognegs_rows = lognegs_bytes.rearrange("(c p t) s -> c p t s", p=P, t=PACK)
    readout_rows = readout.rearrange("(g p t) s -> g p t s", p=P, t=PACK)
    back_rows = back.rearrange("(g p t) n -> g p t n", p=P, t=PACK)

    with ExitStack() as ctx:
        keep = ctx.enter_context(tc.tile_pool(name="keep", bufs=1))
        ring = ctx.enter_context(tc.tile_pool(name="ring", bufs=8))
        work = ctx.enter_context(tc.tile_pool(name="work", bufs=2))
        psum = ctx.enter_context(tc.psum_pool(name="psum", bufs=8))
        ctx.enter_context(tc.manual_schedule())

        def operand(name):
            return (
                keep.tile([P, BANK], U32, name=name + "_codes", align_bytes=64),
                keep.tile([P, BANK], U8, name=name + "_scales", align_bytes=64),
            )

        identity = keep.tile([P, P], F32, name="identity")
        zeros = keep.tile([P, BANK], BF16, name="zeros")
        first_sigmoid = keep.tile([P, 1], F32, name="first_sigmoid")
        scale = keep.tile([P, ITEM_PASSES, PACK], F32, name="scale")
        midpoint_raw = keep.tile([P, POOL_PASSES, PACK], BF16, name="midpoint_raw")
        midpoint_f32 = keep.tile([P, POOL_TILES], F32, name="midpoint_f32")
        lognegs_raw = [keep.tile([P, PACK, SCENARIOS], U8, name=f"lognegs_raw{c}", align_bytes=64) for c in range(ITEM_PASSES)]
        readout_raw = [keep.tile([P, PACK, SCENARIOS], BF16, name=f"readout_raw{g}") for g in range(POOL_PASSES)]
        back_raw = {
            (g, x): keep.tile([P, PACK, 2 * BANK], BF16, name=f"back_raw{g}{x}") for x in range(2) for g in range(POOL_PASSES)
        }

        design_mx = [operand(f"design_mx{r}") for r in range(POOL_TILES)]
        lognegs_mx = {(c, h): operand(f"lognegs_mx{c}{h}") for c in range(ITEM_PASSES) for h in range(HALVES)}
        h_mx = {(g, h): operand(f"h_mx{g}{h}") for g in range(POOL_PASSES) for h in range(HALVES)}
        back_mx = {(g, q): operand(f"back_mx{g}{q}") for g in range(POOL_PASSES) for q in range(ITEM_GROUPS)}

        live = {}

        def quantise(mx, grouped):
            nc.vector.quantize_mx(
                out=mx[0][:].bitcast(FP8X4), scales=mx[1][:], in_=grouped[:].rearrange("p n t -> p (n t)")
            )

        def copy_on(engine, dst, src):
            (nc.scalar.copy if engine == "S" else nc.vector.tensor_copy)(out=dst, in_=src)

        def load_lognegs(c, parts):
            for i in range(parts):
                places = slice(i * PACK // parts, (i + 1) * PACK // parts)
                nc.sync.dma_start(out=lognegs_raw[c][:, places, :], in_=lognegs_rows[c][:, places, :])

        def load_design(r):
            rows = ring.tile([P, ITEMS], BF16, name="design_raw", tag="ring")
            nc.sync.dma_start(out=rows[:], in_=design_rows[r // PACK][:, r % PACK, :])
            live["design", r] = rows

        def load_midpoint():
            nc.sync.dma_start(out=midpoint_raw[:], in_=midpoint.rearrange("(g p t) -> p g t", p=P, t=PACK))
            nc.gpsimd.tensor_copy(out=midpoint_f32[:], in_=midpoint_raw[:].rearrange("p g t -> p (g t)"))

        def load_back(g, x):
            nc.sync.dma_start(out=back_raw[g, x][:], in_=back_rows[g][:, :, x * 2 * BANK : (x + 1) * 2 * BANK])

        def warm_up(bank, count):
            for i in range(count):
                nc.tensor.matmul(bank, lhsT=zeros[:, :P], rhs=zeros[:], start=True, stop=True)

        def transpose_design(r, warm_ups):
            words = live.pop(("design", r))[:].bitcast(F32)
            for b in range(2):
                bank = psum.tile([P, 2, 2, P], F32, name="bank")
                if b == 0:
                    warm_up(bank[:].rearrange("p c u m -> p (c u m)"), warm_ups)
                for i in range(2):
                    for u in range(2):
                        first = 2 * P * (2 * b + i) + u
                        nc.tensor.transpose(bank[:, i, u, :], words[:, first : first + 2 * P - 1 : 2], identity[:])
                live["transposed", r, b] = bank

        def group_design(r):
            grouped = work.tile([P, BANK, PACK], BF16, name="design_grouped", align_bytes=64)
            words = grouped[:].rearrange("p n t -> p (n t)").bitcast(F32)
            for b in range(2):
                nc.scalar.copy(
                    out=words[:, BANK * b : BANK * (b + 1)].rearrange("p (c m u) -> p c m u", c=2, u=2),
                    in_=live.pop(("transposed", r, b))[:].rearrange("p c u m -> p c m u"),
                )
            live["design", r] = grouped

        def quantise_design(r):
            quantise(design_mx[r], live.pop(("design", r)))

        def widen_lognegs(c, h):
            pairs = work.tile([P, 2, BANK, 2], BF16, name="lognegs_pairs", bufs=3)
            for t in range(PACK):
                nc.vector.tensor_scalar(
                    out=pairs[:, t // 2, :, t % 2],
                    in0=lognegs_raw[c][:, t, h * BANK : (h + 1) * BANK].bitcast(FP8),
                    scalar1=scale[:, c, t : t + 1],
                    scalar2=None,
                    op0=ALU.mult,
                )
            live["pairs", c, h] = pairs

        def group_lognegs(c, h):
            grouped = work.tile([P, BANK, PACK], BF16, name="lognegs_grouped", align_bytes=64)
            nc.scalar.copy(
                out=grouped[:].rearrange("p n t -> p (n t)").bitcast(F32).rearrange("p (n j) -> p n j", j=2),
                in_=live.pop(("pairs", c, h))[:].rearrange("p j n e -> p (j n e)").bitcast(F32).rearrange("p (j n) -> p n j", j=2),
            )
            live["lognegs", c, h] = grouped

        def quantise_lognegs(c, h):
            quantise(lognegs_mx[c, h], live.pop(("lognegs", c, h)))

        def first_product(r, h):
            bank = psum.tile([P, BANK], F32, name="bank")
            codes, scales = design_mx[r]
            for c in range(ITEM_PASSES):
                cols = slice(c * P, (c + 1) * P)
                nc.tensor.matmul_mx(
                    out=bank[:],
                    lhsT=codes[:, cols].bitcast(FP8X4),
                    lhsT_scale=scales[:, cols],
                    rhs=lognegs_mx[c, h][0][:].bitcast(FP8X4),
                    rhs_scale=lognegs_mx[c, h][1][:],
                    start=c == 0,
                    stop=c == ITEM_PASSES - 1,
                )
            g, t = divmod(r, PACK)
            if t == 0:
                live["chance", g, h] = work.tile([P, PACK, BANK], F32, name="chance")
            nc.scalar.activation(
                out=live["chance", g, h][:, t, :], in_=bank[:], func=ACT.Sigmoid, bias=midpoint_f32[:, r : r + 1]
            )

        def multiply_readout(g, h, x):
            if x == 0:
                live["h", g, h] = work.tile([P, BANK, PACK], BF16, name="h_grouped", align_bytes=64)
            width = BANK // 2
            cols = slice(x * width, (x + 1) * width)
            first = h * BANK + x * width
            nc.vector.tensor_tensor(
                out=live["h", g, h][:, cols, :].rearrange("p (n i) t -> p n t i", i=8),
                in0=live["chance", g, h][:, :, cols].rearrange("p t (n i) -> p n t i", i=8),
                in1=readout_raw[g][:, :, first : first + width].rearrange("p t (n i) -> p n t i", i=8),
                op=ALU.mult,
            )

        def quantise_h(g, h):
            quantise(h_mx[g, h], live.pop(("h", g, h)))

        def group_back(g, q, engine):
            grouped = work.tile([P, BANK, PACK], BF16, name="back_grouped", align_bytes=64, bufs=3)
            first = q % 2 * BANK
            copy_on(
                engine,
                grouped[:].rearrange("p (n i) t -> p n t i", i=4),
                back_raw[g, q // 2][:, :, first : first + BANK].rearrange("p t (n i) -> p n t i", i=4),
            )
            live["back", g, q] = grouped

        def quantise_back(g, q):
            quantise(back_mx[g, q], live.pop(("back", g, q)))

        def second_product(n, h, engine, warm_ups=0):
            bank = psum.tile([P, BANK], F32, name="bank")
            warm_up(bank[:], warm_ups)
            q, j = divmod(n, GROUP)
            cols = slice(j * P, (j + 1) * P)
            for g in range(POOL_PASSES):
                codes, scales = back_mx[g, q]
                nc.tensor.matmul_mx(
                    out=bank[:],
                    lhsT=codes[:, cols].bitcast(FP8X4),
                    lhsT_scale=scales[:, cols],
                    rhs=h_mx[g, h][0][:].bitcast(FP8X4),
                    rhs_scale=h_mx[g, h][1][:],
                    start=g == 0,
                    stop=g == POOL_PASSES - 1,
                )
            rows, half = slice(n * P, (n + 1) * P), slice(h * BANK, (h + 1) * BANK)
            whole_rows = q >= 2 and n != LAST_ITEM_TILE
            if not whole_rows:
                result = ring.tile([P, BANK], F32, name="result", tag="ring")
                copy_on(engine, result[:], bank[:])
                nc.sync.dma_start(out=out[rows, half], in_=result[:])
            else:
                if h == 0:
                    live["out", n] = ring.tile([P, SCENARIOS], F32, name="result_rows", tag="ring")
                copy_on(engine, live["out", n][:, half], bank[:])
                if h == 1:
                    nc.sync.dma_start(out=out[rows, :], in_=live.pop(("out", n))[:])

        make_identity(nc, identity[:])
        nc.vector.memset(first_sigmoid[:], 0.0)
        nc.vector.memset(zeros[:], 0.0)
        nc.scalar.dma_start(out=scale[:], in_=lognegs_scale.rearrange("(c p t) o -> p c (t o)", p=P, t=PACK))
        nc.scalar.activation(out=first_sigmoid[:], in_=first_sigmoid[:], func=ACT.Sigmoid)

        for c in range(ITEM_PASSES):
            load_lognegs(c, 2 if c == 0 else 1)
            load_design(c)
        load_midpoint()
        for r in range(ITEM_PASSES, POOL_TILES):
            load_design(r)
        for g in range(POOL_PASSES):
            nc.sync.dma_start(out=readout_raw[g][:], in_=readout_rows[g])
        for x in range(2):
            for g in range(POOL_PASSES):
                load_back(g, x)

        for c in range(5):
            if c < 4:
                widen_lognegs(c, 0)
            if c > 0:
                group_lognegs(c - 1, 0)
            if c < 4:
                transpose_design(c, 8 if c == 0 else 2)
                group_design(c)
            if c > 0:
                quantise_design(c - 1)
                quantise_lognegs(c - 1, 0)

        for r in range(4, 6):
            transpose_design(r, 1)
            group_design(r)
        for c in range(4):
            widen_lognegs(c, 1)
            first_product(c, 0)
            if c < 2:
                transpose_design(6 + c, 0)
                group_design(6 + c)
            quantise_design(4 + c)
            group_lognegs(c, 1)
            if c > 0:
                quantise_lognegs(c - 1, 1)
        quantise_lognegs(3, 1)
        for r in range(4, 8):
            first_product(r, 0)

        for x in range(2):
            multiply_readout(0, 0, x)
        group_back(0, 0, "S")
        for x in range(2):
            multiply_readout(1, 0, x)
        quantise_h(0, 0)
        quantise_h(1, 0)
        group_back(1, 0, "V")
        for r in range(4):
            first_product(r, 1)
        quantise_back(0, 0)
        group_back(0, 1, "S")
        quantise_back(1, 0)
        group_back(1, 1, "V")
        for r in range(4, 8):
            first_product(r, 1)

        for n in range(0, 4):
            second_product(n, 0, "S")
        for g in range(POOL_PASSES):
            quantise_back(g, 1)
            multiply_readout(0, 1, g)
        for n in range(4, 8):
            second_product(n, 0, "S")
        for x in range(2):
            multiply_readout(1, 1, x)
        quantise_h(0, 1)
        quantise_h(1, 1)
        for n in range(8):
            second_product(n, 1, "S", 6 if n == 0 else 0)

        for q in range(2, 4):
            for g in range(POOL_PASSES):
                group_back(g, q, "V")
            for g in range(POOL_PASSES):
                quantise_back(g, q)
            for n in range(GROUP * q, GROUP * (q + 1)):
                second_product(n, 0, "V" if q == 3 else "S")
                second_product(n, 1, "S")
